import numpy as np
import ml_dtypes


def mxq(x, axis, fmt="e4m3"):
    dtype, down = {"e4m3": (ml_dtypes.float8_e4m3fn, 7), "e5m2": (ml_dtypes.float8_e5m2, 14)}[fmt]
    v = np.moveaxis(np.asarray(x, np.float32).astype(ml_dtypes.bfloat16).astype(np.float64), axis, -1)
    blocks = v.reshape(v.shape[:-1] + (-1, 32))
    amax = np.abs(blocks).max(-1, keepdims=True)
    byte = np.maximum(np.where(amax > 0, np.frexp(amax)[1] - 1 + 127, 0) - down, 1)
    scale = np.exp2(byte - 127.0)
    codes = (blocks / scale).astype(np.float32).astype(dtype).astype(np.float64)
    return np.moveaxis((codes * scale).reshape(v.shape), -1, axis)


WIDE = False


def mx_kscale(k):
    if not WIDE:
        return np.ones(k)
    levels = np.array([10, -10, 5, -5, 0])
    if k % 512:
        return np.exp2(np.random.permutation(np.resize(levels, k // 32))).repeat(32)
    a = np.empty((k // 512, 16))
    for p in range(k // 512):
        a[p, :8] = np.random.permutation(np.resize(levels, 8))
        for g in range(8):
            far = levels[np.abs(levels - a[p, g]) >= 10]
            a[p, g + 8] = far[np.random.randint(len(far))]
    return np.exp2(a.ravel()).repeat(32)


def f64(x):
    return np.asarray(x).astype(np.float64)


def striped(idx):
    return np.tile(idx.reshape(-1, 16).T, (8, 1)).astype(np.uint16)


def unstriped(offs):
    return offs[:16].T.reshape(-1).astype(np.int64)


def pack_weight(w):
    k, n = w.shape
    w = f64(np.asarray(w, np.float32).astype(ml_dtypes.bfloat16)).reshape(k // 32, 32, n)
    amax = np.abs(w).max(1)
    byte = np.clip(np.where(amax > 0, np.frexp(amax)[1] - 1 + 127 - 7, 1), 1, 254)
    scaled = (w * np.exp2(127.0 - byte)[:, None, :]).reshape(k, n).astype(np.float32)
    words = np.ascontiguousarray(scaled.reshape(k // 512, 128, 4, n).transpose(0, 1, 3, 2)).astype(ml_dtypes.float8_e4m3fn).view(np.uint8)
    return words, np.ascontiguousarray(byte.astype(np.uint8).reshape(k // 512, 16, n))


def unpack_weight(words, scales):
    g, p, n, _ = words.shape
    vals = np.ascontiguousarray(words).view(ml_dtypes.float8_e4m3fn).astype(np.float64) * np.repeat(np.exp2(scales.astype(np.float64) - 127.0), 8, axis=1)[..., None]
    return vals.transpose(0, 1, 3, 2).reshape(g * 512, n)


K, T, S, V, N = 512, 4096, 1024, 512, 256


def setup_inputs():
    n = np.random.standard_normal
    s = mx_kscale(K)[:, None]
    packed_xT = pack_weight(n((K, T)) * s)
    return {
        "x_words": packed_xT[0],
        "x_scales": packed_xT[1],
        "w1": (n((K, N)) / np.sqrt(K) / s).astype(np.float32),
        "offs": striped(np.random.permutation(T)[:S]),
        "pos1": striped(np.random.permutation(S)[:V]),
        "pos2": striped(np.random.permutation(S)[:V]),
        "pos3": striped(np.random.permutation(S)[:V]),
    }


def reference(x_words, x_scales, w1, offs, pos1, pos2, pos3):
    xq = unpack_weight(x_words, x_scales)[:, unstriped(offs)]
    y = mxq(f64(w1), 0, "e4m3").T @ xq
    n0 = y[:, unstriped(pos1)]
    n1 = y[:, unstriped(pos2)]
    n2 = y[:, unstriped(pos3)]
    return np.maximum(np.minimum(n0, n1), np.minimum(np.maximum(n0, n1), n2))

@@ -1,0 +1,122 @@
+from contextlib import ExitStack
+
+import concourse.mybir as mybir
+
+K, T, S, V, N = 512, 4096, 1024, 512, 256
+FLOPS = 2 * K * N * S
+
+F32 = mybir.dt.float32
+BF16 = mybir.dt.bfloat16
+I32 = mybir.dt.int32
+U32 = mybir.dt.uint32
+U16 = mybir.dt.uint16
+U8 = mybir.dt.uint8
+FP8X4 = mybir.dt.float8_e4m3fn_x4
+MAX = mybir.AluOpType.max
+MIN = mybir.AluOpType.min
+
+P = 128
+PACK = 4
+HALF = S // 2
+
+
+def tile_picked_median_none_p_kernel(tc, x_words, x_scales, w1, offs, pos1, pos2, pos3, out):
+    nc = tc.nc
+    with ExitStack() as ctx:
+        sb = ctx.enter_context(tc.tile_pool(name="sb", bufs=1))
+        ps = ctx.enter_context(tc.psum_pool(name="ps", bufs=1))
+
+        offs_sb = sb.tile([P, S // 16], U16, name="offs_sb")
+        pos_sb = [sb.tile([P, V // 16], U16, name=f"pos_sb{i}") for i in range(3)]
+        scale_table = sb.tile([P, T], U8, name="scale_table", align_bytes=64)
+        word_table = sb.tile([P, T], I32, name="word_table", align_bytes=64)
+        w_raw = [sb.tile([P, PACK, P], F32, name=f"w_raw{b}", align_bytes=64) for b in range(2)]
+        w_bf = [sb.tile([P, P, PACK], BF16, name=f"w_bf{b}", align_bytes=64) for b in range(2)]
+        w_codes = [sb.tile([P, P], U32, name=f"w_codes{b}", align_bytes=64) for b in range(2)]
+        w_scales = [sb.tile([P, P], U8, name=f"w_scales{b}", align_bytes=64) for b in range(2)]
+        picked_scales = sb.tile([P, S], U8, name="picked_scales", align_bytes=64)
+        x_plane = sb.tile([P, S], U8, name="x_plane", align_bytes=64)
+        x_codes = [sb.tile([P, HALF], U32, name=f"x_codes{h}", align_bytes=64) for h in range(2)]
+        y = [sb.tile([P, S], F32, name=f"y{b}", align_bytes=64) for b in range(2)]
+
+        w_view = w1.rearrange("(p j) n -> p j n", j=PACK)
+
+        scale_table_words = scale_table[:].bitcast(I32)
+        nc.vector.memset(scale_table_words[:, 0:640], 0)
+        nc.gpsimd.memset(scale_table_words[:, 640:1024], 0)
+        nc.sync.dma_start(offs_sb[:], offs)
+        nc.sync.dma_start(w_raw[0][:], w_view[:, :, 0:P])
+        nc.sync.dma_start(pos_sb[0][:], pos1)
+        nc.sync.dma_start(pos_sb[1][:], pos2)
+        nc.sync.dma_start(pos_sb[2][:], pos3)
+        nc.sync.dma_start(scale_table[0:P:8, :].bitcast(I32), x_scales[0].bitcast(I32))
+        nc.sync.dma_start(word_table[:], x_words[0].rearrange("p c r -> p (c r)").bitcast(I32))
+        nc.sync.dma_start(w_raw[1][:], w_view[:, :, P:2 * P])
+
+        def cast_w(b):
+            nc.scalar.copy(w_bf[b][:], w_raw[b][:].rearrange("p j n -> p n j"))
+
+        def quantize_w(b):
+            nc.vector.quantize_mx(out=w_codes[b][:].bitcast(FP8X4), scales=w_scales[b][:],
+                                  in_=w_bf[b][:].rearrange("p n j -> p (n j)"))
+
+        cast_w(0)
+        nc.vector.tensor_copy(picked_scales[:], scale_table[:].indirect(offs_sb[:]))
+        nc.vector.tensor_copy(x_plane[:].bitcast(I32), picked_scales[:].bitcast(I32))
+        for r in range(1, PACK):
+            nc.scalar.dma_start(x_plane[r:P:32, :].bitcast(I32), picked_scales[8 * r:P:32, :].bitcast(I32))
+        quantize_w(0)
+
+        for h in range(2):
+            nc.vector.tensor_copy(x_codes[h][:], word_table[:].bitcast(U32).indirect(offs_sb[:, h * 32:(h + 1) * 32]))
+
+        def product(b, c0, n, copier):
+            h, o = divmod(c0, HALF)
+            acc = ps.tile([P, n], F32, name=f"acc{b}_{c0}")
+            nc.tensor.matmul_mx(out=acc[:], lhsT=w_codes[b][:].bitcast(FP8X4), lhsT_scale=w_scales[b][:],
+                                rhs=x_codes[h][:, o:o + n].bitcast(FP8X4), rhs_scale=x_plane[:, c0:c0 + n],
+                                start=True, stop=True)
+            copier(y[b][:, c0:c0 + n], acc[:])
+
+        product(0, 0, 512, nc.scalar.copy)
+        cast_w(1)
+        product(0, 512, 256, nc.vector.tensor_copy)
+        product(0, 768, 256, nc.scalar.copy)
+        quantize_w(1)
+        product(1, 0, 512, nc.scalar.copy)
+        product(1, 512, 512, nc.scalar.copy)
+
+        g = [[sb.tile([P, V], F32, name=f"g{b}_{i}", align_bytes=64) for i in range(3)] for b in range(2)]
+        hi = [sb.tile([P, V], F32, name=f"hi{b}", align_bytes=64) for b in range(2)]
+        lo = [sb.tile([P, V], F32, name=f"lo{b}", align_bytes=64) for b in range(2)]
+        cap = [sb.tile([P, V], F32, name=f"cap{b}", align_bytes=64) for b in range(2)]
+        med = [sb.tile([P, V], F32, name=f"med{b}", align_bytes=64) for b in range(2)]
+
+        def gather(b, i):
+            nc.vector.tensor_copy(g[b][i][:], y[b][:].indirect(pos_sb[i][:]))
+
+        def pair(b):
+            nc.vector.tensor_tensor(hi[b][:], g[b][0][:], g[b][1][:], MAX)
+            nc.vector.tensor_tensor(lo[b][:], g[b][0][:], g[b][1][:], MIN)
+
+        def capped(b, cols):
+            nc.vector.tensor_tensor(cap[b][:, cols], hi[b][:, cols], g[b][2][:, cols], MIN)
+
+        def median(b, cols, queue):
+            nc.vector.tensor_tensor(med[b][:, cols], lo[b][:, cols], cap[b][:, cols], MAX)
+            queue.dma_start(out[b * P:(b + 1) * P, cols], med[b][:, cols])
+
+        whole, first, second = slice(0, V), slice(0, V // 2), slice(V // 2, V)
+        for i in range(3):
+            gather(0, i)
+        pair(0)
+        capped(0, whole)
+        gather(1, 0)
+        median(0, whole, nc.sync)
+        gather(1, 1)
+        gather(1, 2)
+        pair(1)
+        capped(1, first)
+        capped(1, second)
+        median(1, first, nc.scalar)
+        median(1, second, nc.sync)

@@ -34,8 +34,8 @@ def tile_picked_median_none_p_kernel(tc, x_words, x_scales, w1, offs, pos1, pos2
         w_bf = [sb.tile([P, P, PACK], BF16, name=f"w_bf{b}", align_bytes=64) for b in range(2)]
         w_codes = [sb.tile([P, P], U32, name=f"w_codes{b}", align_bytes=64) for b in range(2)]
         w_scales = [sb.tile([P, P], U8, name=f"w_scales{b}", align_bytes=64) for b in range(2)]
-        picked_scales = sb.tile([P, S], U8, name="picked_scales", align_bytes=64)
-        x_plane = sb.tile([P, S], U8, name="x_plane", align_bytes=64)
+        picked_scales = [sb.tile([P, HALF], U8, name=f"picked_scales{h}", align_bytes=64) for h in range(2)]
+        x_plane = [sb.tile([P, HALF], U8, name=f"x_plane{h}", align_bytes=64) for h in range(2)]
         x_codes = [sb.tile([P, HALF], U32, name=f"x_codes{h}", align_bytes=64) for h in range(2)]
         y = [sb.tile([P, S], F32, name=f"y{b}", align_bytes=64) for b in range(2)]
 
@@ -61,10 +61,11 @@ def tile_picked_median_none_p_kernel(tc, x_words, x_scales, w1, offs, pos1, pos2
                                   in_=w_bf[b][:].rearrange("p n j -> p (n j)"))
 
         cast_w(0)
-        nc.vector.tensor_copy(picked_scales[:], scale_table[:].indirect(offs_sb[:]))
-        nc.vector.tensor_copy(x_plane[:].bitcast(I32), picked_scales[:].bitcast(I32))
-        for r in range(1, PACK):
-            nc.scalar.dma_start(x_plane[r:P:32, :].bitcast(I32), picked_scales[8 * r:P:32, :].bitcast(I32))
+        for h in range(2):
+            nc.vector.tensor_copy(picked_scales[h][:], scale_table[:].indirect(offs_sb[:, h * 32:(h + 1) * 32]))
+            nc.vector.tensor_copy(x_plane[h][:].bitcast(I32), picked_scales[h][:].bitcast(I32))
+            for r in range(1, PACK):
+                nc.scalar.dma_start(x_plane[h][r:P:32, :].bitcast(I32), picked_scales[h][8 * r:P:32, :].bitcast(I32))
         quantize_w(0)
 
         for h in range(2):
@@ -74,7 +75,7 @@ def tile_picked_median_none_p_kernel(tc, x_words, x_scales, w1, offs, pos1, pos2
             h, o = divmod(c0, HALF)
             acc = ps.tile([P, n], F32, name=f"acc{b}_{c0}")
             nc.tensor.matmul_mx(out=acc[:], lhsT=w_codes[b][:].bitcast(FP8X4), lhsT_scale=w_scales[b][:],
-                                rhs=x_codes[h][:, o:o + n].bitcast(FP8X4), rhs_scale=x_plane[:, c0:c0 + n],
+                                rhs=x_codes[h][:, o:o + n].bitcast(FP8X4), rhs_scale=x_plane[h][:, o:o + n],
                                 start=True, stop=True)
             copier(y[b][:, c0:c0 + n], acc[:])
 

@@ -18,6 +18,7 @@ MIN = mybir.AluOpType.min
 P = 128
 PACK = 4
 HALF = S // 2
+ROW0 = P - 16
 
 
 def tile_picked_median_none_p_kernel(tc, x_words, x_scales, w1, offs, pos1, pos2, pos3, out):
@@ -34,24 +35,23 @@ def tile_picked_median_none_p_kernel(tc, x_words, x_scales, w1, offs, pos1, pos2
         w_bf = [sb.tile([P, P, PACK], BF16, name=f"w_bf{b}", align_bytes=64) for b in range(2)]
         w_codes = [sb.tile([P, P], U32, name=f"w_codes{b}", align_bytes=64) for b in range(2)]
         w_scales = [sb.tile([P, P], U8, name=f"w_scales{b}", align_bytes=64) for b in range(2)]
-        picked_scales = [sb.tile([P, HALF], U8, name=f"picked_scales{h}", align_bytes=64) for h in range(2)]
-        x_plane = [sb.tile([P, HALF], U8, name=f"x_plane{h}", align_bytes=64) for h in range(2)]
+        picked_scales = sb.tile([P, S], U8, name="picked_scales", align_bytes=64)
+        x_plane = sb.tile([P, S], U8, name="x_plane", align_bytes=64)
         x_codes = [sb.tile([P, HALF], U32, name=f"x_codes{h}", align_bytes=64) for h in range(2)]
         y = [sb.tile([P, S], F32, name=f"y{b}", align_bytes=64) for b in range(2)]
 
         w_view = w1.rearrange("(p j) n -> p j n", j=PACK)
 
-        scale_table_words = scale_table[:].bitcast(I32)
-        nc.vector.memset(scale_table_words[:, 0:640], 0)
-        nc.gpsimd.memset(scale_table_words[:, 640:1024], 0)
+        nc.sync.dma_start(scale_table[ROW0:P, :].bitcast(I32), x_scales[0].bitcast(I32))
         nc.sync.dma_start(offs_sb[:], offs)
         nc.sync.dma_start(w_raw[0][:], w_view[:, :, 0:P])
         nc.sync.dma_start(pos_sb[0][:], pos1)
-        nc.sync.dma_start(pos_sb[1][:], pos2)
-        nc.sync.dma_start(pos_sb[2][:], pos3)
-        nc.sync.dma_start(scale_table[0:P:8, :].bitcast(I32), x_scales[0].bitcast(I32))
         nc.sync.dma_start(word_table[:], x_words[0].rearrange("p c r -> p (c r)").bitcast(I32))
         nc.sync.dma_start(w_raw[1][:], w_view[:, :, P:2 * P])
+        nc.sync.dma_start(pos_sb[1][:], pos2)
+        nc.sync.dma_start(pos_sb[2][:], pos3)
+        nc.vector.memset(scale_table[0:ROW0, :].bitcast(I32), 0)
+        nc.vector.memset(x_plane[:].bitcast(I32), 0)
 
         def cast_w(b):
             nc.scalar.copy(w_bf[b][:], w_raw[b][:].rearrange("p j n -> p n j"))
@@ -61,11 +61,10 @@ def tile_picked_median_none_p_kernel(tc, x_words, x_scales, w1, offs, pos1, pos2
                                   in_=w_bf[b][:].rearrange("p n j -> p (n j)"))
 
         cast_w(0)
-        for h in range(2):
-            nc.vector.tensor_copy(picked_scales[h][:], scale_table[:].indirect(offs_sb[:, h * 32:(h + 1) * 32]))
-            nc.vector.tensor_copy(x_plane[h][:].bitcast(I32), picked_scales[h][:].bitcast(I32))
-            for r in range(1, PACK):
-                nc.scalar.dma_start(x_plane[h][r:P:32, :].bitcast(I32), picked_scales[h][8 * r:P:32, :].bitcast(I32))
+        nc.vector.tensor_copy(picked_scales[:], scale_table[:].indirect(offs_sb[:]))
+        for q in range(4):
+            nc.scalar.dma_start(x_plane[32 * q:32 * q + 4, :].bitcast(I32),
+                                picked_scales[ROW0 + 4 * q:ROW0 + 4 * q + 4, :].bitcast(I32))
         quantize_w(0)
 
         for h in range(2):
@@ -75,7 +74,7 @@ def tile_picked_median_none_p_kernel(tc, x_words, x_scales, w1, offs, pos1, pos2
             h, o = divmod(c0, HALF)
             acc = ps.tile([P, n], F32, name=f"acc{b}_{c0}")
             nc.tensor.matmul_mx(out=acc[:], lhsT=w_codes[b][:].bitcast(FP8X4), lhsT_scale=w_scales[b][:],
-                                rhs=x_codes[h][:, o:o + n].bitcast(FP8X4), rhs_scale=x_plane[h][:, o:o + n],
+                                rhs=x_codes[h][:, o:o + n].bitcast(FP8X4), rhs_scale=x_plane[:, c0:c0 + n],
                                 start=True, stop=True)
             copier(y[b][:, c0:c0 + n], acc[:])
 

@@ -44,7 +44,7 @@ def tile_picked_median_none_p_kernel(tc, x_words, x_scales, w1, offs, pos1, pos2
 
         nc.sync.dma_start(scale_table[ROW0:P, :].bitcast(I32), x_scales[0].bitcast(I32))
         nc.sync.dma_start(offs_sb[:], offs)
-        nc.sync.dma_start(w_raw[0][:], w_view[:, :, 0:P])
+        nc.scalar.dma_start(w_raw[0][:], w_view[:, :, 0:P])
         nc.sync.dma_start(pos_sb[0][:], pos1)
         nc.sync.dma_start(word_table[:], x_words[0].rearrange("p c r -> p (c r)").bitcast(I32))
         nc.sync.dma_start(w_raw[1][:], w_view[:, :, P:2 * P])
@@ -81,7 +81,8 @@ def tile_picked_median_none_p_kernel(tc, x_words, x_scales, w1, offs, pos1, pos2
         product(0, 0, 512, nc.scalar.copy)
         cast_w(1)
         product(0, 512, 256, nc.vector.tensor_copy)
-        product(0, 768, 256, nc.scalar.copy)
+        product(0, 768, 128, nc.scalar.copy)
+        product(0, 896, 128, nc.scalar.copy)
         quantize_w(1)
         product(1, 0, 512, nc.scalar.copy)
         product(1, 512, 512, nc.scalar.copy)

@@ -45,9 +45,9 @@ def tile_picked_median_none_p_kernel(tc, x_words, x_scales, w1, offs, pos1, pos2
         nc.sync.dma_start(scale_table[ROW0:P, :].bitcast(I32), x_scales[0].bitcast(I32))
         nc.sync.dma_start(offs_sb[:], offs)
         nc.scalar.dma_start(w_raw[0][:], w_view[:, :, 0:P])
-        nc.sync.dma_start(pos_sb[0][:], pos1)
         nc.sync.dma_start(word_table[:], x_words[0].rearrange("p c r -> p (c r)").bitcast(I32))
         nc.sync.dma_start(w_raw[1][:], w_view[:, :, P:2 * P])
+        nc.sync.dma_start(pos_sb[0][:], pos1)
         nc.sync.dma_start(pos_sb[1][:], pos2)
         nc.sync.dma_start(pos_sb[2][:], pos3)
         nc.vector.memset(scale_table[0:ROW0, :].bitcast(I32), 0)
@@ -78,8 +78,9 @@ def tile_picked_median_none_p_kernel(tc, x_words, x_scales, w1, offs, pos1, pos2
                                 start=True, stop=True)
             copier(y[b][:, c0:c0 + n], acc[:])
 
-        product(0, 0, 512, nc.scalar.copy)
         cast_w(1)
+        product(0, 0, 256, nc.scalar.copy)
+        product(0, 256, 256, nc.scalar.copy)
         product(0, 512, 256, nc.vector.tensor_copy)
         product(0, 768, 128, nc.scalar.copy)
         product(0, 896, 128, nc.scalar.copy)

@@ -14,11 +14,16 @@ U8 = mybir.dt.uint8
 FP8X4 = mybir.dt.float8_e4m3fn_x4
 MAX = mybir.AluOpType.max
 MIN = mybir.AluOpType.min
+ADD = mybir.AluOpType.add
+SUB = mybir.AluOpType.subtract
+MULT = mybir.AluOpType.mult
+ACT = mybir.ActivationFunctionType
 
 P = 128
 PACK = 4
 HALF = S // 2
 ROW0 = P - 16
+MASKED = 192
 
 
 def tile_picked_median_none_p_kernel(tc, x_words, x_scales, w1, offs, pos1, pos2, pos3, out):
@@ -88,37 +93,52 @@ def tile_picked_median_none_p_kernel(tc, x_words, x_scales, w1, offs, pos1, pos2
         product(1, 0, 512, nc.scalar.copy)
         product(1, 512, 512, nc.scalar.copy)
 
-        g = [[sb.tile([P, V], F32, name=f"g{b}_{i}", align_bytes=64) for i in range(3)] for b in range(2)]
-        hi = [sb.tile([P, V], F32, name=f"hi{b}", align_bytes=64) for b in range(2)]
-        lo = [sb.tile([P, V], F32, name=f"lo{b}", align_bytes=64) for b in range(2)]
-        cap = [sb.tile([P, V], F32, name=f"cap{b}", align_bytes=64) for b in range(2)]
-        med = [sb.tile([P, V], F32, name=f"med{b}", align_bytes=64) for b in range(2)]
+        W = 2 * V
+        ab = sb.tile([P, 2, W], F32, name="ab", align_bytes=64)
+        c = sb.tile([P, W], F32, name="c", align_bytes=64)
+        hi_lo = sb.tile([P, 2, W], F32, name="hi_lo", align_bytes=64)
+        cap = sb.tile([P, W], F32, name="cap", align_bytes=64)
+        med = sb.tile([P, W], F32, name="med", align_bytes=64)
 
-        def gather(b, i):
-            nc.vector.tensor_copy(g[b][i][:], y[b][:].indirect(pos_sb[i][:]))
+        def gather(i, c0, c1):
+            b, v0 = divmod(c0, V)
+            dst = c[:, c0:c1] if i == 2 else ab[:, i, c0:c1]
+            nc.vector.tensor_copy(dst, y[b][:].indirect(pos_sb[i][:, v0 // 16:(v0 + c1 - c0) // 16]))
 
-        def pair(b):
-            nc.vector.tensor_tensor(hi[b][:], g[b][0][:], g[b][1][:], MAX)
-            nc.vector.tensor_tensor(lo[b][:], g[b][0][:], g[b][1][:], MIN)
-
-        def capped(b, cols):
-            nc.vector.tensor_tensor(cap[b][:, cols], hi[b][:, cols], g[b][2][:, cols], MIN)
-
-        def median(b, cols, queue):
-            nc.vector.tensor_tensor(med[b][:, cols], lo[b][:, cols], cap[b][:, cols], MAX)
-            queue.dma_start(out[b * P:(b + 1) * P, cols], med[b][:, cols])
-
-        whole, first, second = slice(0, V), slice(0, V // 2), slice(V // 2, V)
+        for c0, c1 in ((0, MASKED), (MASKED, V)):
+            gather(0, c0, c1)
+            gather(1, c0, c1)
+        gather(2, 0, V)
         for i in range(3):
-            gather(0, i)
-        pair(0)
-        capped(0, whole)
-        gather(1, 0)
-        median(0, whole, nc.sync)
-        gather(1, 1)
-        gather(1, 2)
-        pair(1)
-        capped(1, first)
-        capped(1, second)
-        median(1, first, nc.scalar)
-        median(1, second, nc.sync)
+            gather(i, V, W)
+
+        diff = sb.tile([P, MASKED], F32, name="diff", align_bytes=64)
+        order = sb.tile([P, MASKED], F32, name="order", align_bytes=64)
+        picks = sb.tile([P, 3, MASKED], F32, name="picks", align_bytes=64)
+        terms = sb.tile([P, 2, 2, MASKED], F32, name="terms", align_bytes=64)
+        nc.gpsimd.tensor_tensor(diff[:], ab[:, 0, 0:MASKED], ab[:, 1, 0:MASKED], SUB)
+        nc.scalar.activation(order[:], diff[:], ACT.Sign)
+        nc.scalar.activation(picks[:, 0, :], order[:], ACT.Relu)
+        nc.scalar.activation(picks[:, 1, :], order[:], ACT.Sign, bias=1.0, scale=-1.0)
+        nc.scalar.activation(picks[:, 2, :], order[:], ACT.Relu)
+        for i in range(2):
+            nc.gpsimd.tensor_tensor(terms[:, i, :, :], ab[:, :, 0:MASKED], picks[:, i:i + 2, :], MULT)
+        nc.gpsimd.tensor_tensor(hi_lo[:, :, 0:MASKED], terms[:, :, 0, :], terms[:, :, 1, :], ADD)
+
+        nc.vector.tensor_tensor(hi_lo[:, 0, MASKED:], ab[:, 0, MASKED:], ab[:, 1, MASKED:], MAX)
+        nc.vector.tensor_tensor(hi_lo[:, 1, MASKED:], ab[:, 0, MASKED:], ab[:, 1, MASKED:], MIN)
+
+        def capped(c0, n):
+            nc.vector.tensor_tensor(cap[:, c0:c0 + n], hi_lo[:, 0, c0:c0 + n], c[:, c0:c0 + n], MIN)
+
+        def median(c0, n, queue):
+            nc.vector.tensor_tensor(med[:, c0:c0 + n], hi_lo[:, 1, c0:c0 + n], cap[:, c0:c0 + n], MAX)
+            b, v0 = divmod(c0, V)
+            queue.dma_start(out[b * P:(b + 1) * P, v0:v0 + n], med[:, c0:c0 + n])
+
+        capped(0, V)
+        capped(V, V // 2)
+        median(0, V, nc.sync)
+        capped(V + V // 2, V // 2)
+        median(V, V // 2, nc.scalar)
+        median(V + V // 2, V // 2, nc.sync)

@@ -14,22 +14,22 @@ U8 = mybir.dt.uint8
 FP8X4 = mybir.dt.float8_e4m3fn_x4
 MAX = mybir.AluOpType.max
 MIN = mybir.AluOpType.min
-ADD = mybir.AluOpType.add
 SUB = mybir.AluOpType.subtract
 MULT = mybir.AluOpType.mult
-ACT = mybir.ActivationFunctionType
+SIGN = mybir.ActivationFunctionType.Sign
 
 P = 128
 PACK = 4
 HALF = S // 2
 ROW0 = P - 16
-MASKED = 192
+SIGNED = 256
 
 
 def tile_picked_median_none_p_kernel(tc, x_words, x_scales, w1, offs, pos1, pos2, pos3, out):
     nc = tc.nc
     with ExitStack() as ctx:
         sb = ctx.enter_context(tc.tile_pool(name="sb", bufs=1))
+        reused = ctx.enter_context(tc.tile_pool(name="reused", bufs=1))
         ps = ctx.enter_context(tc.psum_pool(name="ps", bufs=1))
 
         offs_sb = sb.tile([P, S // 16], U16, name="offs_sb")
@@ -94,51 +94,53 @@ def tile_picked_median_none_p_kernel(tc, x_words, x_scales, w1, offs, pos1, pos2
         product(1, 512, 512, nc.scalar.copy)
 
         W = 2 * V
-        ab = sb.tile([P, 2, W], F32, name="ab", align_bytes=64)
-        c = sb.tile([P, W], F32, name="c", align_bytes=64)
-        hi_lo = sb.tile([P, 2, W], F32, name="hi_lo", align_bytes=64)
+        wide = W - SIGNED
+        hi_lo_bytes = 2 * wide * 4
+        abc = sb.tile([P, 3, W], F32, name="abc", align_bytes=64)
+        diff = sb.tile([P, SIGNED], F32, name="diff", align_bytes=64)
+        sign3 = sb.tile([P, SIGNED], F32, name="sign3", align_bytes=64)
+        sign_in = reused.tile([P, SIGNED], F32, name="sign_in", offset=hi_lo_bytes - 64, align_bytes=64)
+        sign_out = sb.tile([P, SIGNED], F32, name="sign_out", align_bytes=64)
+        turned = sb.tile([P, 3, SIGNED], F32, name="turned", align_bytes=64)
+        turned_cap = sb.tile([P, SIGNED], F32, name="turned_cap", align_bytes=64)
+        turned_med = sb.tile([P, SIGNED], F32, name="turned_med", align_bytes=64)
         cap = sb.tile([P, W], F32, name="cap", align_bytes=64)
         med = sb.tile([P, W], F32, name="med", align_bytes=64)
 
-        def gather(i, c0, c1):
-            b, v0 = divmod(c0, V)
-            dst = c[:, c0:c1] if i == 2 else ab[:, i, c0:c1]
-            nc.vector.tensor_copy(dst, y[b][:].indirect(pos_sb[i][:, v0 // 16:(v0 + c1 - c0) // 16]))
+        def gather(dst, b, i, v0, v1):
+            nc.vector.tensor_copy(dst, y[b][:].indirect(pos_sb[i][:, v0 // 16:v1 // 16]))
 
-        for c0, c1 in ((0, MASKED), (MASKED, V)):
-            gather(0, c0, c1)
-            gather(1, c0, c1)
-        gather(2, 0, V)
-        for i in range(3):
-            gather(i, V, W)
-
-        diff = sb.tile([P, MASKED], F32, name="diff", align_bytes=64)
-        order = sb.tile([P, MASKED], F32, name="order", align_bytes=64)
-        picks = sb.tile([P, 3, MASKED], F32, name="picks", align_bytes=64)
-        terms = sb.tile([P, 2, 2, MASKED], F32, name="terms", align_bytes=64)
-        nc.gpsimd.tensor_tensor(diff[:], ab[:, 0, 0:MASKED], ab[:, 1, 0:MASKED], SUB)
-        nc.scalar.activation(order[:], diff[:], ACT.Sign)
-        nc.scalar.activation(picks[:, 0, :], order[:], ACT.Relu)
-        nc.scalar.activation(picks[:, 1, :], order[:], ACT.Sign, bias=1.0, scale=-1.0)
-        nc.scalar.activation(picks[:, 2, :], order[:], ACT.Relu)
         for i in range(2):
-            nc.gpsimd.tensor_tensor(terms[:, i, :, :], ab[:, :, 0:MASKED], picks[:, i:i + 2, :], MULT)
-        nc.gpsimd.tensor_tensor(hi_lo[:, :, 0:MASKED], terms[:, :, 0, :], terms[:, :, 1, :], ADD)
+            gather(abc[:, i, 0:SIGNED], 0, i, 0, SIGNED)
+        gather(abc[:, 2, 0:V], 0, 2, 0, V)
+        nc.gpsimd.tensor_tensor(diff[:], abc[:, 1, 0:SIGNED], abc[:, 0, 0:SIGNED], SUB)
+        nc.scalar.activation(sign3[:], diff[:], SIGN)
+        nc.scalar.activation(sign_in[:], sign3[:], SIGN, bias=0.5)
+        nc.scalar.activation(sign_out[:], sign3[:], SIGN, bias=0.5)
+        nc.gpsimd.tensor_tensor(turned[:], abc[:, :, 0:SIGNED],
+                                sign_in[:].unsqueeze(1).to_broadcast([P, 3, SIGNED]), MULT)
+        for i in range(2):
+            gather(abc[:, i, SIGNED:V], 0, i, SIGNED, V)
+        for i in range(2):
+            gather(abc[:, i, V:W], 1, i, 0, V)
 
-        nc.vector.tensor_tensor(hi_lo[:, 0, MASKED:], ab[:, 0, MASKED:], ab[:, 1, MASKED:], MAX)
-        nc.vector.tensor_tensor(hi_lo[:, 1, MASKED:], ab[:, 0, MASKED:], ab[:, 1, MASKED:], MIN)
+        hi_lo = reused.tile([P, 2, wide], F32, name="hi_lo", offset=0, align_bytes=64)
+        c_last = reused.tile([P, V], F32, name="c_last", offset=hi_lo_bytes, align_bytes=64)
+        rest = V - SIGNED
+        nc.vector.tensor_tensor(turned_cap[:], turned[:, 1, :], turned[:, 2, :], MIN)
+        nc.vector.tensor_tensor(hi_lo[:, 0, :], abc[:, 0, SIGNED:W], abc[:, 1, SIGNED:W], MAX)
+        nc.vector.tensor_tensor(turned_med[:], turned[:, 0, :], turned_cap[:], MAX)
+        nc.vector.tensor_tensor(hi_lo[:, 1, :], abc[:, 0, SIGNED:W], abc[:, 1, SIGNED:W], MIN)
+        nc.vector.tensor_tensor(cap[:, SIGNED:V], hi_lo[:, 0, 0:rest], abc[:, 2, SIGNED:V], MIN)
+        gather(c_last[:], 1, 2, 0, V)
+        nc.gpsimd.tensor_tensor(med[:, 0:SIGNED], turned_med[:], sign_out[:], MULT)
+        nc.vector.tensor_tensor(med[:, SIGNED:V], hi_lo[:, 1, 0:rest], cap[:, SIGNED:V], MAX)
+        nc.sync.dma_start(out[0:P, :], med[:, 0:V])
 
-        def capped(c0, n):
-            nc.vector.tensor_tensor(cap[:, c0:c0 + n], hi_lo[:, 0, c0:c0 + n], c[:, c0:c0 + n], MIN)
-
-        def median(c0, n, queue):
-            nc.vector.tensor_tensor(med[:, c0:c0 + n], hi_lo[:, 1, c0:c0 + n], cap[:, c0:c0 + n], MAX)
-            b, v0 = divmod(c0, V)
-            queue.dma_start(out[b * P:(b + 1) * P, v0:v0 + n], med[:, c0:c0 + n])
-
-        capped(0, V)
-        capped(V, V // 2)
-        median(0, V, nc.sync)
-        capped(V + V // 2, V // 2)
-        median(V, V // 2, nc.scalar)
-        median(V + V // 2, V // 2, nc.sync)
+        halves = [h * V // 2 for h in range(2)]
+        n = V // 2
+        for v0 in halves:
+            nc.vector.tensor_tensor(cap[:, V + v0:V + v0 + n], hi_lo[:, 0, rest + v0:rest + v0 + n], c_last[:, v0:v0 + n], MIN)
+        for v0, queue in zip(halves, (nc.scalar, nc.sync)):
+            nc.vector.tensor_tensor(med[:, V + v0:V + v0 + n], hi_lo[:, 1, rest + v0:rest + v0 + n], cap[:, V + v0:V + v0 + n], MAX)
+            queue.dma_start(out[P:2 * P, v0:v0 + n], med[:, V + v0:V + v0 + n])

@@ -22,7 +22,8 @@ P = 128
 PACK = 4
 HALF = S // 2
 ROW0 = P - 16
-SIGNED = 256
+SIGNED = 288
+TIE_SCALE, TIE_BIAS = 2.0 ** 30, 2.0 ** -120
 
 
 def tile_picked_median_none_p_kernel(tc, x_words, x_scales, w1, offs, pos1, pos2, pos3, out):
@@ -52,9 +53,9 @@ def tile_picked_median_none_p_kernel(tc, x_words, x_scales, w1, offs, pos1, pos2
         nc.scalar.dma_start(w_raw[0][:], w_view[:, :, 0:P])
         nc.sync.dma_start(word_table[:], x_words[0].rearrange("p c r -> p (c r)").bitcast(I32))
         nc.sync.dma_start(w_raw[1][:], w_view[:, :, P:2 * P])
-        nc.sync.dma_start(pos_sb[0][:], pos1)
-        nc.sync.dma_start(pos_sb[1][:], pos2)
-        nc.sync.dma_start(pos_sb[2][:], pos3)
+        nc.sync.dma_start(pos_sb[0][:], pos2)
+        nc.sync.dma_start(pos_sb[1][:], pos3)
+        nc.sync.dma_start(pos_sb[2][:], pos1)
         nc.vector.memset(scale_table[0:ROW0, :].bitcast(I32), 0)
         nc.vector.memset(x_plane[:].bitcast(I32), 0)
 
@@ -98,7 +99,6 @@ def tile_picked_median_none_p_kernel(tc, x_words, x_scales, w1, offs, pos1, pos2
         hi_lo_bytes = 2 * wide * 4
         abc = sb.tile([P, 3, W], F32, name="abc", align_bytes=64)
         diff = sb.tile([P, SIGNED], F32, name="diff", align_bytes=64)
-        sign3 = sb.tile([P, SIGNED], F32, name="sign3", align_bytes=64)
         sign_in = reused.tile([P, SIGNED], F32, name="sign_in", offset=hi_lo_bytes - 64, align_bytes=64)
         sign_out = sb.tile([P, SIGNED], F32, name="sign_out", align_bytes=64)
         turned = sb.tile([P, 3, SIGNED], F32, name="turned", align_bytes=64)
@@ -114,9 +114,8 @@ def tile_picked_median_none_p_kernel(tc, x_words, x_scales, w1, offs, pos1, pos2
             gather(abc[:, i, 0:SIGNED], 0, i, 0, SIGNED)
         gather(abc[:, 2, 0:V], 0, 2, 0, V)
         nc.gpsimd.tensor_tensor(diff[:], abc[:, 1, 0:SIGNED], abc[:, 0, 0:SIGNED], SUB)
-        nc.scalar.activation(sign3[:], diff[:], SIGN)
-        nc.scalar.activation(sign_in[:], sign3[:], SIGN, bias=0.5)
-        nc.scalar.activation(sign_out[:], sign3[:], SIGN, bias=0.5)
+        nc.scalar.activation(sign_in[:], diff[:], SIGN, bias=TIE_BIAS, scale=TIE_SCALE)
+        nc.scalar.activation(sign_out[:], diff[:], SIGN, bias=TIE_BIAS, scale=TIE_SCALE)
         nc.gpsimd.tensor_tensor(turned[:], abc[:, :, 0:SIGNED],
                                 sign_in[:].unsqueeze(1).to_broadcast([P, 3, SIGNED]), MULT)
         for i in range(2):

@@ -35,9 +35,9 @@ def tile_picked_median_none_p_kernel(tc, x_words, x_scales, w1, offs, pos1, pos2
 
         offs_sb = sb.tile([P, S // 16], U16, name="offs_sb")
         pos_sb = [sb.tile([P, V // 16], U16, name=f"pos_sb{i}") for i in range(3)]
-        scale_table = sb.tile([P, T], U8, name="scale_table", align_bytes=64)
+        scale_table = sb.tile([P, T], U8, name="scale_table", tag="early_late", align_bytes=64)
         word_table = sb.tile([P, T], I32, name="word_table", align_bytes=64)
-        w_raw = [sb.tile([P, PACK, P], F32, name=f"w_raw{b}", align_bytes=64) for b in range(2)]
+        w_raw = [sb.tile([P, PACK, P], F32, name="w_raw0", align_bytes=64)]
         w_bf = [sb.tile([P, P, PACK], BF16, name=f"w_bf{b}", align_bytes=64) for b in range(2)]
         w_codes = [sb.tile([P, P], U32, name=f"w_codes{b}", align_bytes=64) for b in range(2)]
         w_scales = [sb.tile([P, P], U8, name=f"w_scales{b}", align_bytes=64) for b in range(2)]
@@ -51,9 +51,8 @@ def tile_picked_median_none_p_kernel(tc, x_words, x_scales, w1, offs, pos1, pos2
         nc.sync.dma_start(scale_table[ROW0:P, :].bitcast(I32), x_scales[0].bitcast(I32))
         nc.sync.dma_start(offs_sb[:], offs)
         nc.scalar.dma_start(w_raw[0][:], w_view[:, :, 0:P])
-        nc.sync.dma_start(word_table[:], x_words[0].rearrange("p c r -> p (c r)").bitcast(I32))
-        nc.sync.dma_start(w_raw[1][:], w_view[:, :, P:2 * P])
         nc.sync.dma_start(pos_sb[0][:], pos2)
+        nc.sync.dma_start(word_table[:], x_words[0].rearrange("p c r -> p (c r)").bitcast(I32))
         nc.sync.dma_start(pos_sb[1][:], pos3)
         nc.sync.dma_start(pos_sb[2][:], pos1)
         nc.vector.memset(scale_table[0:ROW0, :].bitcast(I32), 0)
@@ -69,8 +68,10 @@ def tile_picked_median_none_p_kernel(tc, x_words, x_scales, w1, offs, pos1, pos2
         cast_w(0)
         nc.vector.tensor_copy(picked_scales[:], scale_table[:].indirect(offs_sb[:]))
         for q in range(4):
-            nc.scalar.dma_start(x_plane[32 * q:32 * q + 4, :].bitcast(I32),
+            nc.sync.dma_start(x_plane[32 * q:32 * q + 4, :].bitcast(I32),
                                 picked_scales[ROW0 + 4 * q:ROW0 + 4 * q + 4, :].bitcast(I32))
+        w_raw.append(sb.tile([P, PACK, P], F32, name="w_raw1", tag="early_late", align_bytes=64))
+        nc.sync.dma_start(w_raw[1][:], w_view[:, :, P:2 * P])
         quantize_w(0)
 
         for h in range(2):

@@ -51,10 +51,9 @@ def tile_picked_median_none_p_kernel(tc, x_words, x_scales, w1, offs, pos1, pos2
         nc.sync.dma_start(scale_table[ROW0:P, :].bitcast(I32), x_scales[0].bitcast(I32))
         nc.sync.dma_start(offs_sb[:], offs)
         nc.scalar.dma_start(w_raw[0][:], w_view[:, :, 0:P])
-        nc.sync.dma_start(pos_sb[0][:], pos2)
         nc.sync.dma_start(word_table[:], x_words[0].rearrange("p c r -> p (c r)").bitcast(I32))
+        nc.sync.dma_start(pos_sb[0][:], pos2)
         nc.sync.dma_start(pos_sb[1][:], pos3)
-        nc.sync.dma_start(pos_sb[2][:], pos1)
         nc.vector.memset(scale_table[0:ROW0, :].bitcast(I32), 0)
         nc.vector.memset(x_plane[:].bitcast(I32), 0)
 
@@ -72,6 +71,7 @@ def tile_picked_median_none_p_kernel(tc, x_words, x_scales, w1, offs, pos1, pos2
                                 picked_scales[ROW0 + 4 * q:ROW0 + 4 * q + 4, :].bitcast(I32))
         w_raw.append(sb.tile([P, PACK, P], F32, name="w_raw1", tag="early_late", align_bytes=64))
         nc.sync.dma_start(w_raw[1][:], w_view[:, :, P:2 * P])
+        nc.sync.dma_start(pos_sb[2][:], pos1)
         quantize_w(0)
 
         for h in range(2):

@@ -14,23 +14,20 @@ U8 = mybir.dt.uint8
 FP8X4 = mybir.dt.float8_e4m3fn_x4
 MAX = mybir.AluOpType.max
 MIN = mybir.AluOpType.min
-SUB = mybir.AluOpType.subtract
-MULT = mybir.AluOpType.mult
-SIGN = mybir.ActivationFunctionType.Sign
+COPY = mybir.ActivationFunctionType.Copy
 
 P = 128
 PACK = 4
 HALF = S // 2
 ROW0 = P - 16
-SIGNED = 288
-TIE_SCALE, TIE_BIAS = 2.0 ** 30, 2.0 ** -120
+CHUNKS = [(0, 0, 256), (0, 256, 256), (1, 0, 256), (1, 256, 128), (1, 384, 128)]
+VECTOR_GATHERS = {(1, 2)}
 
 
 def tile_picked_median_none_p_kernel(tc, x_words, x_scales, w1, offs, pos1, pos2, pos3, out):
     nc = tc.nc
     with ExitStack() as ctx:
         sb = ctx.enter_context(tc.tile_pool(name="sb", bufs=1))
-        reused = ctx.enter_context(tc.tile_pool(name="reused", bufs=1))
         ps = ctx.enter_context(tc.psum_pool(name="ps", bufs=1))
 
         offs_sb = sb.tile([P, S // 16], U16, name="offs_sb")
@@ -52,8 +49,8 @@ def tile_picked_median_none_p_kernel(tc, x_words, x_scales, w1, offs, pos1, pos2
         nc.sync.dma_start(offs_sb[:], offs)
         nc.scalar.dma_start(w_raw[0][:], w_view[:, :, 0:P])
         nc.sync.dma_start(word_table[:], x_words[0].rearrange("p c r -> p (c r)").bitcast(I32))
-        nc.sync.dma_start(pos_sb[0][:], pos2)
-        nc.sync.dma_start(pos_sb[1][:], pos3)
+        nc.sync.dma_start(pos_sb[0][:], pos1)
+        nc.sync.dma_start(pos_sb[1][:], pos2)
         nc.vector.memset(scale_table[0:ROW0, :].bitcast(I32), 0)
         nc.vector.memset(x_plane[:].bitcast(I32), 0)
 
@@ -68,10 +65,10 @@ def tile_picked_median_none_p_kernel(tc, x_words, x_scales, w1, offs, pos1, pos2
         nc.vector.tensor_copy(picked_scales[:], scale_table[:].indirect(offs_sb[:]))
         for q in range(4):
             nc.sync.dma_start(x_plane[32 * q:32 * q + 4, :].bitcast(I32),
-                                picked_scales[ROW0 + 4 * q:ROW0 + 4 * q + 4, :].bitcast(I32))
+                              picked_scales[ROW0 + 4 * q:ROW0 + 4 * q + 4, :].bitcast(I32))
         w_raw.append(sb.tile([P, PACK, P], F32, name="w_raw1", tag="early_late", align_bytes=64))
         nc.sync.dma_start(w_raw[1][:], w_view[:, :, P:2 * P])
-        nc.sync.dma_start(pos_sb[2][:], pos1)
+        nc.sync.dma_start(pos_sb[2][:], pos3)
         quantize_w(0)
 
         for h in range(2):
@@ -92,55 +89,26 @@ def tile_picked_median_none_p_kernel(tc, x_words, x_scales, w1, offs, pos1, pos2
         product(0, 768, 128, nc.scalar.copy)
         product(0, 896, 128, nc.scalar.copy)
         quantize_w(1)
-        product(1, 0, 512, nc.scalar.copy)
-        product(1, 512, 512, nc.scalar.copy)
+        product(1, 0, 512, nc.vector.tensor_copy)
+        product(1, 512, 512, nc.vector.tensor_copy)
 
-        W = 2 * V
-        wide = W - SIGNED
-        hi_lo_bytes = 2 * wide * 4
-        abc = sb.tile([P, 3, W], F32, name="abc", align_bytes=64)
-        diff = sb.tile([P, SIGNED], F32, name="diff", align_bytes=64)
-        sign_in = reused.tile([P, SIGNED], F32, name="sign_in", offset=hi_lo_bytes - 64, align_bytes=64)
-        sign_out = sb.tile([P, SIGNED], F32, name="sign_out", align_bytes=64)
-        turned = sb.tile([P, 3, SIGNED], F32, name="turned", align_bytes=64)
-        turned_cap = sb.tile([P, SIGNED], F32, name="turned_cap", align_bytes=64)
-        turned_med = sb.tile([P, SIGNED], F32, name="turned_med", align_bytes=64)
-        cap = sb.tile([P, W], F32, name="cap", align_bytes=64)
-        med = sb.tile([P, W], F32, name="med", align_bytes=64)
-
-        def gather(dst, b, i, v0, v1):
-            nc.vector.tensor_copy(dst, y[b][:].indirect(pos_sb[i][:, v0 // 16:v1 // 16]))
-
-        for i in range(2):
-            gather(abc[:, i, 0:SIGNED], 0, i, 0, SIGNED)
-        gather(abc[:, 2, 0:V], 0, 2, 0, V)
-        nc.gpsimd.tensor_tensor(diff[:], abc[:, 1, 0:SIGNED], abc[:, 0, 0:SIGNED], SUB)
-        nc.scalar.activation(sign_in[:], diff[:], SIGN, bias=TIE_BIAS, scale=TIE_SCALE)
-        nc.scalar.activation(sign_out[:], diff[:], SIGN, bias=TIE_BIAS, scale=TIE_SCALE)
-        nc.gpsimd.tensor_tensor(turned[:], abc[:, :, 0:SIGNED],
-                                sign_in[:].unsqueeze(1).to_broadcast([P, 3, SIGNED]), MULT)
-        for i in range(2):
-            gather(abc[:, i, SIGNED:V], 0, i, SIGNED, V)
-        for i in range(2):
-            gather(abc[:, i, V:W], 1, i, 0, V)
-
-        hi_lo = reused.tile([P, 2, wide], F32, name="hi_lo", offset=0, align_bytes=64)
-        c_last = reused.tile([P, V], F32, name="c_last", offset=hi_lo_bytes, align_bytes=64)
-        rest = V - SIGNED
-        nc.vector.tensor_tensor(turned_cap[:], turned[:, 1, :], turned[:, 2, :], MIN)
-        nc.vector.tensor_tensor(hi_lo[:, 0, :], abc[:, 0, SIGNED:W], abc[:, 1, SIGNED:W], MAX)
-        nc.vector.tensor_tensor(turned_med[:], turned[:, 0, :], turned_cap[:], MAX)
-        nc.vector.tensor_tensor(hi_lo[:, 1, :], abc[:, 0, SIGNED:W], abc[:, 1, SIGNED:W], MIN)
-        nc.vector.tensor_tensor(cap[:, SIGNED:V], hi_lo[:, 0, 0:rest], abc[:, 2, SIGNED:V], MIN)
-        gather(c_last[:], 1, 2, 0, V)
-        nc.gpsimd.tensor_tensor(med[:, 0:SIGNED], turned_med[:], sign_out[:], MULT)
-        nc.vector.tensor_tensor(med[:, SIGNED:V], hi_lo[:, 1, 0:rest], cap[:, SIGNED:V], MAX)
-        nc.sync.dma_start(out[0:P, :], med[:, 0:V])
-
-        halves = [h * V // 2 for h in range(2)]
-        n = V // 2
-        for v0 in halves:
-            nc.vector.tensor_tensor(cap[:, V + v0:V + v0 + n], hi_lo[:, 0, rest + v0:rest + v0 + n], c_last[:, v0:v0 + n], MIN)
-        for v0, queue in zip(halves, (nc.scalar, nc.sync)):
-            nc.vector.tensor_tensor(med[:, V + v0:V + v0 + n], hi_lo[:, 1, rest + v0:rest + v0 + n], cap[:, V + v0:V + v0 + n], MAX)
-            queue.dma_start(out[P:2 * P, v0:v0 + n], med[:, V + v0:V + v0 + n])
+        med = [sb.tile([P, V], F32, name=f"med{b}", align_bytes=64) for b in range(2)]
+        for c, (b, v0, n) in enumerate(CHUNKS):
+            nb = [sb.tile([P, n], F32, name=f"nb{c}_{i}", align_bytes=64) for i in range(3)]
+            hi = sb.tile([P, n], F32, name=f"hi{c}", align_bytes=64)
+            lo = sb.tile([P, n], F32, name=f"lo{c}", align_bytes=64)
+            cap = sb.tile([P, n], F32, name=f"cap{c}", align_bytes=64)
+            for i in range(3):
+                picked = y[b][:].indirect(pos_sb[i][:, v0 // 16:(v0 + n) // 16])
+                if (c, i) in VECTOR_GATHERS:
+                    nc.vector.tensor_copy(nb[i][:], picked)
+                else:
+                    nc.scalar.activation(nb[i][:], picked, COPY)
+            nc.vector.tensor_tensor(hi[:], nb[0][:], nb[1][:], MAX)
+            nc.vector.tensor_tensor(lo[:], nb[0][:], nb[1][:], MIN)
+            nc.vector.tensor_tensor(cap[:], hi[:], nb[2][:], MIN)
+            nc.vector.tensor_tensor(med[b][:, v0:v0 + n], lo[:], cap[:], MAX)
+            if b == 1:
+                nc.sync.dma_start(out[P:2 * P, v0:v0 + n], med[1][:, v0:v0 + n])
+            elif v0 + n == V:
+                nc.sync.dma_start(out[0:P, :], med[0][:])

@@ -18,10 +18,8 @@ COPY = mybir.ActivationFunctionType.Copy
 
 P = 128
 PACK = 4
-HALF = S // 2
 ROW0 = P - 16
-CHUNKS = [(0, 0, 256), (0, 256, 256), (1, 0, 256), (1, 256, 128), (1, 384, 128)]
-VECTOR_GATHERS = {(1, 2)}
+QUARTER = S // 4
 
 
 def tile_picked_median_none_p_kernel(tc, x_words, x_scales, w1, offs, pos1, pos2, pos3, out):
@@ -32,83 +30,105 @@ def tile_picked_median_none_p_kernel(tc, x_words, x_scales, w1, offs, pos1, pos2
 
         offs_sb = sb.tile([P, S // 16], U16, name="offs_sb")
         pos_sb = [sb.tile([P, V // 16], U16, name=f"pos_sb{i}") for i in range(3)]
-        scale_table = sb.tile([P, T], U8, name="scale_table", tag="early_late", align_bytes=64)
+        scale_table = sb.tile([P, T], U8, name="scale_table", align_bytes=64)
         word_table = sb.tile([P, T], I32, name="word_table", align_bytes=64)
-        w_raw = [sb.tile([P, PACK, P], F32, name="w_raw0", align_bytes=64)]
-        w_bf = [sb.tile([P, P, PACK], BF16, name=f"w_bf{b}", align_bytes=64) for b in range(2)]
-        w_codes = [sb.tile([P, P], U32, name=f"w_codes{b}", align_bytes=64) for b in range(2)]
-        w_scales = [sb.tile([P, P], U8, name=f"w_scales{b}", align_bytes=64) for b in range(2)]
+        w_raw = sb.tile([P, PACK, N], F32, name="w_raw", align_bytes=64)
+        w_bf = sb.tile([P, N, PACK], BF16, name="w_bf", align_bytes=64)
+        w_codes = sb.tile([P, N], U32, name="w_codes", align_bytes=64)
+        w_scales = sb.tile([P, N], U8, name="w_scales", align_bytes=64)
         picked_scales = sb.tile([P, S], U8, name="picked_scales", align_bytes=64)
         x_plane = sb.tile([P, S], U8, name="x_plane", align_bytes=64)
-        x_codes = [sb.tile([P, HALF], U32, name=f"x_codes{h}", align_bytes=64) for h in range(2)]
+        x_codes = [sb.tile([P, QUARTER], U32, name=f"x_codes{h}", align_bytes=64) for h in range(4)]
         y = [sb.tile([P, S], F32, name=f"y{b}", align_bytes=64) for b in range(2)]
-
-        w_view = w1.rearrange("(p j) n -> p j n", j=PACK)
 
         nc.sync.dma_start(scale_table[ROW0:P, :].bitcast(I32), x_scales[0].bitcast(I32))
         nc.sync.dma_start(offs_sb[:], offs)
-        nc.scalar.dma_start(w_raw[0][:], w_view[:, :, 0:P])
+        nc.scalar.dma_start(w_raw[:], w1.rearrange("(p j) n -> p j n", j=PACK))
         nc.sync.dma_start(word_table[:], x_words[0].rearrange("p c r -> p (c r)").bitcast(I32))
         nc.sync.dma_start(pos_sb[0][:], pos1)
         nc.sync.dma_start(pos_sb[1][:], pos2)
         nc.vector.memset(scale_table[0:ROW0, :].bitcast(I32), 0)
         nc.vector.memset(x_plane[:].bitcast(I32), 0)
 
-        def cast_w(b):
-            nc.scalar.copy(w_bf[b][:], w_raw[b][:].rearrange("p j n -> p n j"))
-
-        def quantize_w(b):
-            nc.vector.quantize_mx(out=w_codes[b][:].bitcast(FP8X4), scales=w_scales[b][:],
-                                  in_=w_bf[b][:].rearrange("p n j -> p (n j)"))
-
-        cast_w(0)
+        nc.scalar.copy(w_bf[:], w_raw[:].rearrange("p j n -> p n j"))
         nc.vector.tensor_copy(picked_scales[:], scale_table[:].indirect(offs_sb[:]))
         for q in range(4):
             nc.sync.dma_start(x_plane[32 * q:32 * q + 4, :].bitcast(I32),
                               picked_scales[ROW0 + 4 * q:ROW0 + 4 * q + 4, :].bitcast(I32))
-        w_raw.append(sb.tile([P, PACK, P], F32, name="w_raw1", tag="early_late", align_bytes=64))
-        nc.sync.dma_start(w_raw[1][:], w_view[:, :, P:2 * P])
         nc.sync.dma_start(pos_sb[2][:], pos3)
-        quantize_w(0)
+        nc.vector.quantize_mx(out=w_codes[:].bitcast(FP8X4), scales=w_scales[:],
+                              in_=w_bf[:].rearrange("p n j -> p (n j)"))
 
-        for h in range(2):
-            nc.vector.tensor_copy(x_codes[h][:], word_table[:].bitcast(U32).indirect(offs_sb[:, h * 32:(h + 1) * 32]))
+        for h in range(4):
+            nc.vector.tensor_copy(x_codes[h][:], word_table[:].bitcast(U32).indirect(offs_sb[:, h * 16:(h + 1) * 16]))
 
         def product(b, c0, n, copier):
-            h, o = divmod(c0, HALF)
-            acc = ps.tile([P, n], F32, name=f"acc{b}_{c0}")
-            nc.tensor.matmul_mx(out=acc[:], lhsT=w_codes[b][:].bitcast(FP8X4), lhsT_scale=w_scales[b][:],
+            h, o = divmod(c0, QUARTER)
+            acc = ps.tile([P, n], F32, name=f"acc{b}_{c0}", tag=f"bank{(2 * (c0 // QUARTER) + b + 2 * (c0 // 896)) % 8}")
+            nc.tensor.matmul_mx(out=acc[:], lhsT=w_codes[:, b * P:(b + 1) * P].bitcast(FP8X4),
+                                lhsT_scale=w_scales[:, b * P:(b + 1) * P],
                                 rhs=x_codes[h][:, o:o + n].bitcast(FP8X4), rhs_scale=x_plane[:, c0:c0 + n],
                                 start=True, stop=True)
             copier(y[b][:, c0:c0 + n], acc[:])
 
-        cast_w(1)
-        product(0, 0, 256, nc.scalar.copy)
-        product(0, 256, 256, nc.scalar.copy)
-        product(0, 512, 256, nc.vector.tensor_copy)
+        for c0 in range(0, 2 * QUARTER, QUARTER):
+            for b in range(2):
+                product(b, c0, QUARTER, nc.scalar.copy)
+        product(0, 512, 256, nc.scalar.copy)
+        product(1, 512, 256, nc.vector.tensor_copy)
         product(0, 768, 128, nc.scalar.copy)
-        product(0, 896, 128, nc.scalar.copy)
-        quantize_w(1)
-        product(1, 0, 512, nc.vector.tensor_copy)
-        product(1, 512, 512, nc.vector.tensor_copy)
+        product(0, 896, 128, nc.vector.tensor_copy)
+        product(1, 768, 256, nc.scalar.copy)
 
-        med = [sb.tile([P, V], F32, name=f"med{b}", align_bytes=64) for b in range(2)]
-        for c, (b, v0, n) in enumerate(CHUNKS):
-            nb = [sb.tile([P, n], F32, name=f"nb{c}_{i}", align_bytes=64) for i in range(3)]
-            hi = sb.tile([P, n], F32, name=f"hi{c}", align_bytes=64)
-            lo = sb.tile([P, n], F32, name=f"lo{c}", align_bytes=64)
-            cap = sb.tile([P, n], F32, name=f"cap{c}", align_bytes=64)
-            for i in range(3):
-                picked = y[b][:].indirect(pos_sb[i][:, v0 // 16:(v0 + n) // 16])
-                if (c, i) in VECTOR_GATHERS:
-                    nc.vector.tensor_copy(nb[i][:], picked)
-                else:
-                    nc.scalar.activation(nb[i][:], picked, COPY)
-            nc.vector.tensor_tensor(hi[:], nb[0][:], nb[1][:], MAX)
-            nc.vector.tensor_tensor(lo[:], nb[0][:], nb[1][:], MIN)
-            nc.vector.tensor_tensor(cap[:], hi[:], nb[2][:], MIN)
-            nc.vector.tensor_tensor(med[b][:, v0:v0 + n], lo[:], cap[:], MAX)
-            if b == 1:
-                nc.sync.dma_start(out[P:2 * P, v0:v0 + n], med[1][:, v0:v0 + n])
-            elif v0 + n == V:
-                nc.sync.dma_start(out[0:P, :], med[0][:])
+        W = 2 * V
+        nb = [sb.tile([P, W], F32, name=f"nb{i}", align_bytes=64) for i in range(3)]
+        hi, lo, cap, med = (sb.tile([P, W], F32, name=name, align_bytes=64) for name in ("hi", "lo", "cap", "med"))
+
+        def picked(i, c0, c1):
+            b, v0 = divmod(c0, V)
+            return y[b][:].indirect(pos_sb[i][:, v0 // 16:(v0 + c1 - c0) // 16])
+
+        def on_vector(i, c0, c1):
+            nc.vector.tensor_copy(nb[i][:, c0:c1], picked(i, c0, c1))
+
+        def on_scalar(i, c0, c1):
+            nc.scalar.activation(nb[i][:, c0:c1], picked(i, c0, c1), COPY)
+
+        def step(dst, in0, in1, op, c0, c1):
+            nc.vector.tensor_tensor(dst[:, c0:c1], in0[:, c0:c1], in1[:, c0:c1], op)
+
+        def bounds(c0, c1):
+            step(hi, nb[0], nb[1], MAX, c0, c1)
+            step(lo, nb[0], nb[1], MIN, c0, c1)
+
+        def store(c0, c1, queue=nc.sync):
+            b, v0 = divmod(c0, V)
+            queue.dma_start(out[b * P:(b + 1) * P, v0:v0 + c1 - c0], med[:, c0:c1])
+
+        on_vector(0, 0, 512)
+        on_scalar(1, 0, 512)
+        on_vector(0, 512, 768)
+        on_scalar(2, 0, 512)
+        on_scalar(1, 512, 768)
+        on_scalar(0, 896, 1024)
+        on_scalar(1, 768, 1024)
+        on_scalar(2, 512, 768)
+        on_scalar(2, 768, 896)
+        on_scalar(2, 896, 1024)
+        bounds(0, 512)
+        step(cap, hi, nb[2], MIN, 0, 512)
+        on_vector(0, 768, 896)
+        step(hi, nb[0], nb[1], MAX, 512, 768)
+        step(med, lo, cap, MAX, 0, 512)
+        store(0, 512)
+        step(lo, nb[0], nb[1], MIN, 512, 768)
+        bounds(768, 1024)
+        step(cap, hi, nb[2], MIN, 512, 768)
+        step(cap, hi, nb[2], MIN, 768, 896)
+        step(med, lo, cap, MAX, 512, 768)
+        store(512, 768)
+        step(cap, hi, nb[2], MIN, 896, 1024)
+        step(med, lo, cap, MAX, 768, 896)
+        store(768, 896)
+        step(med, lo, cap, MAX, 896, 1024)
+        store(896, 1024, nc.scalar)

@@ -110,23 +110,21 @@ def tile_picked_median_none_p_kernel(tc, x_words, x_scales, w1, offs, pos1, pos2
         on_vector(0, 512, 768)
         on_scalar(2, 0, 512)
         on_scalar(1, 512, 768)
-        on_scalar(0, 896, 1024)
-        on_scalar(1, 768, 1024)
         on_scalar(2, 512, 768)
+        on_scalar(0, 768, 1024)
+        on_scalar(1, 768, 1024)
         on_scalar(2, 768, 896)
         on_scalar(2, 896, 1024)
         bounds(0, 512)
         step(cap, hi, nb[2], MIN, 0, 512)
-        on_vector(0, 768, 896)
-        step(hi, nb[0], nb[1], MAX, 512, 768)
+        bounds(512, 768)
+        step(cap, hi, nb[2], MIN, 512, 768)
         step(med, lo, cap, MAX, 0, 512)
         store(0, 512)
-        step(lo, nb[0], nb[1], MIN, 512, 768)
-        bounds(768, 1024)
-        step(cap, hi, nb[2], MIN, 512, 768)
-        step(cap, hi, nb[2], MIN, 768, 896)
         step(med, lo, cap, MAX, 512, 768)
         store(512, 768)
+        bounds(768, 1024)
+        step(cap, hi, nb[2], MIN, 768, 896)
         step(cap, hi, nb[2], MIN, 896, 1024)
         step(med, lo, cap, MAX, 768, 896)
         store(768, 896)

@@ -18,8 +18,8 @@ COPY = mybir.ActivationFunctionType.Copy
 
 P = 128
 PACK = 4
-ROW0 = P - 16
 QUARTER = S // 4
+ROW0, ROW_STEP = 32, 4
 
 
 def tile_picked_median_none_p_kernel(tc, x_words, x_scales, w1, offs, pos1, pos2, pos3, out):
@@ -41,44 +41,46 @@ def tile_picked_median_none_p_kernel(tc, x_words, x_scales, w1, offs, pos1, pos2
         x_codes = [sb.tile([P, QUARTER], U32, name=f"x_codes{h}", align_bytes=64) for h in range(4)]
         y = [sb.tile([P, S], F32, name=f"y{b}", align_bytes=64) for b in range(2)]
 
-        nc.sync.dma_start(scale_table[ROW0:P, :].bitcast(I32), x_scales[0].bitcast(I32))
-        nc.sync.dma_start(offs_sb[:], offs)
+        nc.vector.memset(scale_table[:].bitcast(I32), 0)
         nc.scalar.dma_start(w_raw[:], w1.rearrange("(p j) n -> p j n", j=PACK))
-        nc.sync.dma_start(word_table[:], x_words[0].rearrange("p c r -> p (c r)").bitcast(I32))
+        nc.sync.dma_start(offs_sb[:], offs)
         nc.sync.dma_start(pos_sb[0][:], pos1)
         nc.sync.dma_start(pos_sb[1][:], pos2)
-        nc.vector.memset(scale_table[0:ROW0, :].bitcast(I32), 0)
+        nc.sync.dma_start(pos_sb[2][:], pos3)
+        nc.sync.dma_start(scale_table[ROW0:ROW0 + 16 * ROW_STEP:ROW_STEP, :].bitcast(I32), x_scales[0].bitcast(I32))
+        nc.sync.dma_start(word_table[:], x_words[0].rearrange("p c r -> p (c r)").bitcast(I32))
         nc.vector.memset(x_plane[:].bitcast(I32), 0)
 
         nc.scalar.copy(w_bf[:], w_raw[:].rearrange("p j n -> p n j"))
         nc.vector.tensor_copy(picked_scales[:], scale_table[:].indirect(offs_sb[:]))
         for q in range(4):
+            r0 = ROW0 + 4 * q * ROW_STEP
             nc.sync.dma_start(x_plane[32 * q:32 * q + 4, :].bitcast(I32),
-                              picked_scales[ROW0 + 4 * q:ROW0 + 4 * q + 4, :].bitcast(I32))
-        nc.sync.dma_start(pos_sb[2][:], pos3)
+                              picked_scales[r0:r0 + 4 * ROW_STEP:ROW_STEP, :].bitcast(I32))
         nc.vector.quantize_mx(out=w_codes[:].bitcast(FP8X4), scales=w_scales[:],
                               in_=w_bf[:].rearrange("p n j -> p (n j)"))
 
         for h in range(4):
             nc.vector.tensor_copy(x_codes[h][:], word_table[:].bitcast(U32).indirect(offs_sb[:, h * 16:(h + 1) * 16]))
 
-        def product(b, c0, n, copier):
+        def product(b, c0, n, bank, copier):
             h, o = divmod(c0, QUARTER)
-            acc = ps.tile([P, n], F32, name=f"acc{b}_{c0}", tag=f"bank{(2 * (c0 // QUARTER) + b + 2 * (c0 // 896)) % 8}")
+            acc = ps.tile([P, n], F32, name=f"acc{b}_{c0}", tag=f"bank{bank}")
             nc.tensor.matmul_mx(out=acc[:], lhsT=w_codes[:, b * P:(b + 1) * P].bitcast(FP8X4),
                                 lhsT_scale=w_scales[:, b * P:(b + 1) * P],
                                 rhs=x_codes[h][:, o:o + n].bitcast(FP8X4), rhs_scale=x_plane[:, c0:c0 + n],
                                 start=True, stop=True)
             copier(y[b][:, c0:c0 + n], acc[:])
 
-        for c0 in range(0, 2 * QUARTER, QUARTER):
-            for b in range(2):
-                product(b, c0, QUARTER, nc.scalar.copy)
-        product(0, 512, 256, nc.scalar.copy)
-        product(1, 512, 256, nc.vector.tensor_copy)
-        product(0, 768, 128, nc.scalar.copy)
-        product(0, 896, 128, nc.vector.tensor_copy)
-        product(1, 768, 256, nc.scalar.copy)
+        product(0, 0, 256, 0, nc.scalar.copy)
+        product(1, 0, 256, 1, nc.scalar.copy)
+        product(0, 256, 256, 2, nc.scalar.copy)
+        product(1, 256, 256, 3, nc.scalar.copy)
+        product(0, 512, 256, 4, nc.scalar.copy)
+        product(1, 512, 256, 5, nc.vector.tensor_copy)
+        product(0, 768, 128, 6, nc.scalar.copy)
+        product(0, 896, 128, 0, nc.vector.tensor_copy)
+        product(1, 768, 256, 7, nc.scalar.copy)
 
         W = 2 * V
         nb = [sb.tile([P, W], F32, name=f"nb{i}", align_bytes=64) for i in range(3)]
@@ -101,7 +103,11 @@ def tile_picked_median_none_p_kernel(tc, x_words, x_scales, w1, offs, pos1, pos2
             step(hi, nb[0], nb[1], MAX, c0, c1)
             step(lo, nb[0], nb[1], MIN, c0, c1)
 
-        def store(c0, c1, queue=nc.sync):
+        def upper(c0, c1):
+            step(cap, hi, nb[2], MIN, c0, c1)
+
+        def finish(c0, c1, queue=nc.sync):
+            step(med, lo, cap, MAX, c0, c1)
             b, v0 = divmod(c0, V)
             queue.dma_start(out[b * P:(b + 1) * P, v0:v0 + c1 - c0], med[:, c0:c1])
 
@@ -116,17 +122,13 @@ def tile_picked_median_none_p_kernel(tc, x_words, x_scales, w1, offs, pos1, pos2
         on_scalar(2, 768, 896)
         on_scalar(2, 896, 1024)
         bounds(0, 512)
-        step(cap, hi, nb[2], MIN, 0, 512)
+        upper(0, 512)
         bounds(512, 768)
-        step(cap, hi, nb[2], MIN, 512, 768)
-        step(med, lo, cap, MAX, 0, 512)
-        store(0, 512)
-        step(med, lo, cap, MAX, 512, 768)
-        store(512, 768)
+        upper(512, 768)
+        finish(0, 512)
+        finish(512, 768)
         bounds(768, 1024)
-        step(cap, hi, nb[2], MIN, 768, 896)
-        step(cap, hi, nb[2], MIN, 896, 1024)
-        step(med, lo, cap, MAX, 768, 896)
-        store(768, 896)
-        step(med, lo, cap, MAX, 896, 1024)
-        store(896, 1024, nc.scalar)
+        upper(768, 896)
+        upper(896, 1024)
+        finish(768, 896)
+        finish(896, 1024, nc.scalar)

@@ -19,7 +19,7 @@ COPY = mybir.ActivationFunctionType.Copy
 P = 128
 PACK = 4
 QUARTER = S // 4
-ROW0, ROW_STEP = 32, 4
+ROW0 = P - 16
 
 
 def tile_picked_median_none_p_kernel(tc, x_words, x_scales, w1, offs, pos1, pos2, pos3, out):
@@ -41,22 +41,21 @@ def tile_picked_median_none_p_kernel(tc, x_words, x_scales, w1, offs, pos1, pos2
         x_codes = [sb.tile([P, QUARTER], U32, name=f"x_codes{h}", align_bytes=64) for h in range(4)]
         y = [sb.tile([P, S], F32, name=f"y{b}", align_bytes=64) for b in range(2)]
 
-        nc.vector.memset(scale_table[:].bitcast(I32), 0)
-        nc.scalar.dma_start(w_raw[:], w1.rearrange("(p j) n -> p j n", j=PACK))
+        nc.sync.dma_start(scale_table[ROW0:P, :].bitcast(I32), x_scales[0].bitcast(I32))
         nc.sync.dma_start(offs_sb[:], offs)
+        nc.scalar.dma_start(w_raw[:], w1.rearrange("(p j) n -> p j n", j=PACK))
+        nc.sync.dma_start(word_table[:], x_words[0].rearrange("p c r -> p (c r)").bitcast(I32))
         nc.sync.dma_start(pos_sb[0][:], pos1)
         nc.sync.dma_start(pos_sb[1][:], pos2)
-        nc.sync.dma_start(pos_sb[2][:], pos3)
-        nc.sync.dma_start(scale_table[ROW0:ROW0 + 16 * ROW_STEP:ROW_STEP, :].bitcast(I32), x_scales[0].bitcast(I32))
-        nc.sync.dma_start(word_table[:], x_words[0].rearrange("p c r -> p (c r)").bitcast(I32))
+        nc.vector.memset(scale_table[0:ROW0, :].bitcast(I32), 0)
         nc.vector.memset(x_plane[:].bitcast(I32), 0)
 
         nc.scalar.copy(w_bf[:], w_raw[:].rearrange("p j n -> p n j"))
         nc.vector.tensor_copy(picked_scales[:], scale_table[:].indirect(offs_sb[:]))
         for q in range(4):
-            r0 = ROW0 + 4 * q * ROW_STEP
             nc.sync.dma_start(x_plane[32 * q:32 * q + 4, :].bitcast(I32),
-                              picked_scales[r0:r0 + 4 * ROW_STEP:ROW_STEP, :].bitcast(I32))
+                              picked_scales[ROW0 + 4 * q:ROW0 + 4 * q + 4, :].bitcast(I32))
+        nc.sync.dma_start(pos_sb[2][:], pos3)
         nc.vector.quantize_mx(out=w_codes[:].bitcast(FP8X4), scales=w_scales[:],
                               in_=w_bf[:].rearrange("p n j -> p (n j)"))
 
@@ -80,7 +79,8 @@ def tile_picked_median_none_p_kernel(tc, x_words, x_scales, w1, offs, pos1, pos2
         product(1, 512, 256, 5, nc.vector.tensor_copy)
         product(0, 768, 128, 6, nc.scalar.copy)
         product(0, 896, 128, 0, nc.vector.tensor_copy)
-        product(1, 768, 256, 7, nc.scalar.copy)
+        product(1, 768, 128, 7, nc.vector.tensor_copy)
+        product(1, 896, 128, 1, nc.scalar.copy)
 
         W = 2 * V
         nb = [sb.tile([P, W], F32, name=f"nb{i}", align_bytes=64) for i in range(3)]
@@ -130,5 +130,5 @@ def tile_picked_median_none_p_kernel(tc, x_words, x_scales, w1, offs, pos1, pos2
         bounds(768, 1024)
         upper(768, 896)
         upper(896, 1024)
-        finish(768, 896)
-        finish(896, 1024, nc.scalar)
+        finish(768, 896, nc.scalar)
+        finish(896, 1024)

@@ -114,21 +114,19 @@ def tile_picked_median_none_p_kernel(tc, x_words, x_scales, w1, offs, pos1, pos2
         on_vector(0, 0, 512)
         on_scalar(1, 0, 512)
         on_vector(0, 512, 768)
-        on_scalar(2, 0, 512)
         on_scalar(1, 512, 768)
-        on_scalar(2, 512, 768)
+        on_scalar(2, 0, 512)
         on_scalar(0, 768, 1024)
         on_scalar(1, 768, 1024)
-        on_scalar(2, 768, 896)
-        on_scalar(2, 896, 1024)
-        bounds(0, 512)
+        on_scalar(2, 512, 768)
+        on_scalar(2, 768, 1024)
+        step(hi, nb[0], nb[1], MAX, 0, 512)
+        step(lo, nb[0], nb[1], MIN, 0, 768)
         upper(0, 512)
-        bounds(512, 768)
-        upper(512, 768)
+        step(hi, nb[0], nb[1], MAX, 512, 768)
         finish(0, 512)
-        finish(512, 768)
         bounds(768, 1024)
-        upper(768, 896)
-        upper(896, 1024)
-        finish(768, 896, nc.scalar)
-        finish(896, 1024)
+        upper(512, 768)
+        upper(768, 1024)
+        finish(512, 768, nc.scalar)
+        finish(768, 1024)

@@ -20,6 +20,10 @@ P = 128
 PACK = 4
 QUARTER = S // 4
 ROW0 = P - 16
+W = 2 * V
+MIDDLE_END = 832
+LAST_CUT = 928
+VECTOR_END = 864
 
 
 def tile_picked_median_none_p_kernel(tc, x_words, x_scales, w1, offs, pos1, pos2, pos3, out):
@@ -82,9 +86,9 @@ def tile_picked_median_none_p_kernel(tc, x_words, x_scales, w1, offs, pos1, pos2
         product(1, 768, 128, 7, nc.vector.tensor_copy)
         product(1, 896, 128, 1, nc.scalar.copy)
 
-        W = 2 * V
-        nb = [sb.tile([P, W], F32, name=f"nb{i}", align_bytes=64) for i in range(3)]
-        hi, lo, cap, med = (sb.tile([P, W], F32, name=name, align_bytes=64) for name in ("hi", "lo", "cap", "med"))
+        left, right, low = (sb.tile([P, 2, W], F32, name=name, align_bytes=64) for name in ("left", "right", "low"))
+        med = sb.tile([P, W], F32, name="med", align_bytes=64)
+        nb = (left[:, 0, :], right[:, 0, :], right[:, 1, :])
 
         def picked(i, c0, c1):
             b, v0 = divmod(c0, V)
@@ -96,37 +100,39 @@ def tile_picked_median_none_p_kernel(tc, x_words, x_scales, w1, offs, pos1, pos2
         def on_scalar(i, c0, c1):
             nc.scalar.activation(nb[i][:, c0:c1], picked(i, c0, c1), COPY)
 
-        def step(dst, in0, in1, op, c0, c1):
-            nc.vector.tensor_tensor(dst[:, c0:c1], in0[:, c0:c1], in1[:, c0:c1], op)
+        def larger(c0, c1):
+            nc.vector.tensor_tensor(left[:, 1, c0:c1], left[:, 0, c0:c1], right[:, 0, c0:c1], MAX)
 
-        def bounds(c0, c1):
-            step(hi, nb[0], nb[1], MAX, c0, c1)
-            step(lo, nb[0], nb[1], MIN, c0, c1)
+        def minimum(row, c0, c1):
+            nc.vector.tensor_tensor(low[:, row, c0:c1], left[:, row, c0:c1], right[:, row, c0:c1], MIN)
 
-        def upper(c0, c1):
-            step(cap, hi, nb[2], MIN, c0, c1)
+        def minima(c0, c1):
+            nc.vector.tensor_tensor(low[:, :, c0:c1], left[:, :, c0:c1], right[:, :, c0:c1], MIN)
 
         def finish(c0, c1, queue=nc.sync):
-            step(med, lo, cap, MAX, c0, c1)
+            nc.vector.tensor_tensor(med[:, c0:c1], low[:, 0, c0:c1], low[:, 1, c0:c1], MAX)
             b, v0 = divmod(c0, V)
             queue.dma_start(out[b * P:(b + 1) * P, v0:v0 + c1 - c0], med[:, c0:c1])
 
-        on_vector(0, 0, 512)
-        on_scalar(1, 0, 512)
-        on_vector(0, 512, 768)
-        on_scalar(1, 512, 768)
-        on_scalar(2, 0, 512)
-        on_scalar(0, 768, 1024)
-        on_scalar(1, 768, 1024)
-        on_scalar(2, 512, 768)
-        on_scalar(2, 768, 1024)
-        step(hi, nb[0], nb[1], MAX, 0, 512)
-        step(lo, nb[0], nb[1], MIN, 0, 768)
-        upper(0, 512)
-        step(hi, nb[0], nb[1], MAX, 512, 768)
-        finish(0, 512)
-        bounds(768, 1024)
-        upper(512, 768)
-        upper(768, 1024)
-        finish(512, 768, nc.scalar)
-        finish(768, 1024)
+        on_vector(0, 0, V)
+        on_scalar(1, 0, V)
+        on_vector(0, V, VECTOR_END)
+        on_scalar(2, 0, V)
+        on_scalar(1, V, MIDDLE_END)
+        on_scalar(2, V, MIDDLE_END)
+        on_scalar(0, VECTOR_END, W)
+        on_scalar(1, MIDDLE_END, W)
+        on_scalar(2, MIDDLE_END, LAST_CUT)
+        on_scalar(2, LAST_CUT, W)
+        larger(0, V)
+        minimum(0, 0, V)
+        minimum(1, 0, V)
+        larger(V, MIDDLE_END)
+        finish(0, V)
+        minima(V, MIDDLE_END)
+        larger(MIDDLE_END, W)
+        finish(V, MIDDLE_END)
+        minima(MIDDLE_END, LAST_CUT)
+        minima(LAST_CUT, W)
+        finish(MIDDLE_END, LAST_CUT, nc.scalar)
+        finish(LAST_CUT, W)

from contextlib import ExitStack

import concourse.mybir as mybir

K, T, S, V, N = 512, 4096, 1024, 512, 256
FLOPS = 2 * K * N * S

F32 = mybir.dt.float32
BF16 = mybir.dt.bfloat16
I32 = mybir.dt.int32
U32 = mybir.dt.uint32
U16 = mybir.dt.uint16
U8 = mybir.dt.uint8
FP8X4 = mybir.dt.float8_e4m3fn_x4
MAX = mybir.AluOpType.max
MIN = mybir.AluOpType.min
COPY = mybir.ActivationFunctionType.Copy

P = 128
PACK = 4
QUARTER = S // 4
ROW0 = P - 16
W = 2 * V
MIDDLE_END = 832
LAST_CUT = 928
VECTOR_END = 864


def tile_picked_median_none_p_kernel(tc, x_words, x_scales, w1, offs, pos1, pos2, pos3, out):
    nc = tc.nc
    with ExitStack() as ctx:
        sb = ctx.enter_context(tc.tile_pool(name="sb", bufs=1))
        ps = ctx.enter_context(tc.psum_pool(name="ps", bufs=1))

        offs_sb = sb.tile([P, S // 16], U16, name="offs_sb")
        pos_sb = [sb.tile([P, V // 16], U16, name=f"pos_sb{i}") for i in range(3)]
        scale_table = sb.tile([P, T], U8, name="scale_table", align_bytes=64)
        word_table = sb.tile([P, T], I32, name="word_table", align_bytes=64)
        w_raw = sb.tile([P, PACK, N], F32, name="w_raw", align_bytes=64)
        w_bf = sb.tile([P, N, PACK], BF16, name="w_bf", align_bytes=64)
        w_codes = sb.tile([P, N], U32, name="w_codes", align_bytes=64)
        w_scales = sb.tile([P, N], U8, name="w_scales", align_bytes=64)
        picked_scales = sb.tile([P, S], U8, name="picked_scales", align_bytes=64)
        x_plane = sb.tile([P, S], U8, name="x_plane", align_bytes=64)
        x_codes = [sb.tile([P, QUARTER], U32, name=f"x_codes{h}", align_bytes=64) for h in range(4)]
        y = [sb.tile([P, S], F32, name=f"y{b}", align_bytes=64) for b in range(2)]

        nc.sync.dma_start(scale_table[ROW0:P, :].bitcast(I32), x_scales[0].bitcast(I32))
        nc.sync.dma_start(offs_sb[:], offs)
        nc.scalar.dma_start(w_raw[:], w1.rearrange("(p j) n -> p j n", j=PACK))
        nc.sync.dma_start(word_table[:], x_words[0].rearrange("p c r -> p (c r)").bitcast(I32))
        nc.sync.dma_start(pos_sb[0][:], pos1)
        nc.sync.dma_start(pos_sb[1][:], pos2)
        nc.vector.memset(scale_table[0:ROW0, :].bitcast(I32), 0)
        nc.vector.memset(x_plane[:].bitcast(I32), 0)

        nc.scalar.copy(w_bf[:], w_raw[:].rearrange("p j n -> p n j"))
        nc.vector.tensor_copy(picked_scales[:], scale_table[:].indirect(offs_sb[:]))
        for q in range(4):
            nc.sync.dma_start(x_plane[32 * q:32 * q + 4, :].bitcast(I32),
                              picked_scales[ROW0 + 4 * q:ROW0 + 4 * q + 4, :].bitcast(I32))
        nc.sync.dma_start(pos_sb[2][:], pos3)
        nc.vector.quantize_mx(out=w_codes[:].bitcast(FP8X4), scales=w_scales[:],
                              in_=w_bf[:].rearrange("p n j -> p (n j)"))

        for h in range(4):
            nc.vector.tensor_copy(x_codes[h][:], word_table[:].bitcast(U32).indirect(offs_sb[:, h * 16:(h + 1) * 16]))

        def product(b, c0, n, bank, copier):
            h, o = divmod(c0, QUARTER)
            acc = ps.tile([P, n], F32, name=f"acc{b}_{c0}", tag=f"bank{bank}")
            nc.tensor.matmul_mx(out=acc[:], lhsT=w_codes[:, b * P:(b + 1) * P].bitcast(FP8X4),
                                lhsT_scale=w_scales[:, b * P:(b + 1) * P],
                                rhs=x_codes[h][:, o:o + n].bitcast(FP8X4), rhs_scale=x_plane[:, c0:c0 + n],
                                start=True, stop=True)
            copier(y[b][:, c0:c0 + n], acc[:])

        product(0, 0, 256, 0, nc.scalar.copy)
        product(1, 0, 256, 1, nc.scalar.copy)
        product(0, 256, 256, 2, nc.scalar.copy)
        product(1, 256, 256, 3, nc.scalar.copy)
        product(0, 512, 256, 4, nc.scalar.copy)
        product(1, 512, 256, 5, nc.vector.tensor_copy)
        product(0, 768, 128, 6, nc.scalar.copy)
        product(0, 896, 128, 0, nc.vector.tensor_copy)
        product(1, 768, 128, 7, nc.vector.tensor_copy)
        product(1, 896, 128, 1, nc.scalar.copy)

        left, right, low = (sb.tile([P, 2, W], F32, name=name, align_bytes=64) for name in ("left", "right", "low"))
        med = sb.tile([P, W], F32, name="med", align_bytes=64)
        nb = (left[:, 0, :], right[:, 0, :], right[:, 1, :])

        def picked(i, c0, c1):
            b, v0 = divmod(c0, V)
            return y[b][:].indirect(pos_sb[i][:, v0 // 16:(v0 + c1 - c0) // 16])

        def on_vector(i, c0, c1):
            nc.vector.tensor_copy(nb[i][:, c0:c1], picked(i, c0, c1))

        def on_scalar(i, c0, c1):
            nc.scalar.activation(nb[i][:, c0:c1], picked(i, c0, c1), COPY)

        def larger(c0, c1):
            nc.vector.tensor_tensor(left[:, 1, c0:c1], left[:, 0, c0:c1], right[:, 0, c0:c1], MAX)

        def minimum(row, c0, c1):
            nc.vector.tensor_tensor(low[:, row, c0:c1], left[:, row, c0:c1], right[:, row, c0:c1], MIN)

        def minima(c0, c1):
            nc.vector.tensor_tensor(low[:, :, c0:c1], left[:, :, c0:c1], right[:, :, c0:c1], MIN)

        def finish(c0, c1, queue=nc.sync):
            nc.vector.tensor_tensor(med[:, c0:c1], low[:, 0, c0:c1], low[:, 1, c0:c1], MAX)
            b, v0 = divmod(c0, V)
            queue.dma_start(out[b * P:(b + 1) * P, v0:v0 + c1 - c0], med[:, c0:c1])

        on_vector(0, 0, V)
        on_scalar(1, 0, V)
        on_vector(0, V, VECTOR_END)
        on_scalar(2, 0, V)
        on_scalar(1, V, MIDDLE_END)
        on_scalar(2, V, MIDDLE_END)
        on_scalar(0, VECTOR_END, W)
        on_scalar(1, MIDDLE_END, W)
        on_scalar(2, MIDDLE_END, LAST_CUT)
        on_scalar(2, LAST_CUT, W)
        larger(0, V)
        minimum(0, 0, V)
        minimum(1, 0, V)
        larger(V, MIDDLE_END)
        finish(0, V)
        minima(V, MIDDLE_END)
        larger(MIDDLE_END, W)
        finish(V, MIDDLE_END)
        minima(MIDDLE_END, LAST_CUT)
        minima(LAST_CUT, W)
        finish(MIDDLE_END, LAST_CUT, nc.scalar)
        finish(LAST_CUT, W)
